import numpy as np
import ml_dtypes


def mxq(x, axis, fmt="e4m3"):
    dtype, down = {"e4m3": (ml_dtypes.float8_e4m3fn, 7), "e5m2": (ml_dtypes.float8_e5m2, 14)}[fmt]
    v = np.moveaxis(np.asarray(x, np.float32).astype(ml_dtypes.bfloat16).astype(np.float64), axis, -1)
    blocks = v.reshape(v.shape[:-1] + (-1, 32))
    amax = np.abs(blocks).max(-1, keepdims=True)
    byte = np.maximum(np.where(amax > 0, np.frexp(amax)[1] - 1 + 127, 0) - down, 1)
    scale = np.exp2(byte - 127.0)
    codes = (blocks / scale).astype(np.float32).astype(dtype).astype(np.float64)
    return np.moveaxis((codes * scale).reshape(v.shape), -1, axis)


WIDE = False


def mx_kscale(k):
    if not WIDE:
        return np.ones(k)
    levels = np.array([10, -10, 5, -5, 0])
    if k % 512:
        return np.exp2(np.random.permutation(np.resize(levels, k // 32))).repeat(32)
    a = np.empty((k // 512, 16))
    for p in range(k // 512):
        a[p, :8] = np.random.permutation(np.resize(levels, 8))
        for g in range(8):
            far = levels[np.abs(levels - a[p, g]) >= 10]
            a[p, g + 8] = far[np.random.randint(len(far))]
    return np.exp2(a.ravel()).repeat(32)


def f64(x):
    return np.asarray(x).astype(np.float64)


def striped8(idx):
    return np.asarray(idx).reshape(8, -1, 16).transpose(0, 2, 1).reshape(128, -1).astype(np.uint16)


def unstriped8(offs):
    return offs.reshape(8, 16, -1).transpose(0, 2, 1).reshape(8, -1).astype(np.int64)


def pick8(x, idx, run):
    r = np.arange(len(x))
    return x[r[:, None], idx[r % (8 * run) // run]]


E2M1 = np.array([0.0, 0.5, 1.0, 1.5, 2.0, 3.0, 4.0, 6.0, -0.0, -0.5, -1.0, -1.5, -2.0, -3.0, -4.0, -6.0])


def pack_weight(w, fmt):
    k, n = w.shape
    w = f64(np.asarray(w, np.float32).astype(ml_dtypes.bfloat16)).reshape(k // 32, 32, n)
    amax = np.abs(w).max(1)
    if fmt == "e4m3":
        byte = np.frexp(amax)[1] - 1 + 127 - 7
    else:
        mant, ex = np.frexp(amax / 6.0)
        byte = np.where(mant > 0.5, ex, ex - 1) + 127
    byte = np.clip(np.where(amax > 0, byte, 1), 1, 254)
    scaled = (w * np.exp2(127.0 - byte)[:, None, :]).reshape(k, n).astype(np.float32)
    by_word = np.ascontiguousarray(scaled.reshape(k // 512, 128, 4, n).transpose(0, 1, 3, 2))
    if fmt == "e4m3":
        words = by_word.astype(ml_dtypes.float8_e4m3fn).view(np.uint8)
    else:
        c = by_word.astype(ml_dtypes.float4_e2m1fn).view(np.uint8) & 0xF
        words = (c[..., 0::2] | (c[..., 1::2] << 4)).reshape(k // 512, 128, 2 * n)
    return np.ascontiguousarray(words), np.ascontiguousarray(byte.astype(np.uint8).reshape(k // 512, 16, n))


def unpack_weight(words, scales, fmt):
    g, _, n = scales.shape
    words = np.ascontiguousarray(words).reshape(g, 128, n, -1)
    if fmt == "e4m3":
        vals = words.view(ml_dtypes.float8_e4m3fn).astype(np.float64)
    else:
        nib = np.empty((g, 128, n, 4), np.uint8)
        nib[..., 0::2] = words & 0xF
        nib[..., 1::2] = words >> 4
        vals = E2M1[nib]
    vals = vals * np.repeat(np.exp2(scales.astype(np.float64) - 127.0), 8, axis=1)[..., None]
    return vals.transpose(0, 1, 3, 2).reshape(g * 512, n)


D, T, Z, I, Q, E = 512, 1024, 1024, 512, 512, 256


def setup_inputs():
    n = np.random.standard_normal
    idx = np.stack([np.random.permutation(T)[:I] for _ in range(8)])
    idx2 = np.stack([np.random.permutation(T)[:I] for _ in range(8)])
    idx3 = np.stack([np.random.permutation(Z)[:I] for _ in range(8)])
    idx4 = np.stack([np.random.permutation(Z)[:I] for _ in range(8)])
    idx5 = np.stack([np.random.permutation(Z)[:I] for _ in range(8)])
    fd = mx_kscale(D)
    fq = mx_kscale(Q)
    cachep = pack_weight(n((D, T)) / fd[:, None], "e4m3")
    mixp = pack_weight(n((Q, E)) * 1.0 / np.sqrt(Q) / fq[:, None], "e2m1")
    return {
        "query": (n((D, Q)) * 1.0 / np.sqrt(D) * fd[:, None]).astype(np.float32),
        "cache_words": cachep[0],
        "cache_scales": cachep[1],
        "rowf": (np.random.uniform(0.5, 2.0, (Q, 1)) * fq[:, None]).astype(np.float32),
        "mix_words": mixp[0],
        "mix_scales": mixp[1],
        "offs": striped8(idx),
        "offs2": striped8(idx2),
        "offs3": striped8(idx3),
        "offs4": striped8(idx4),
        "offs5": striped8(idx5),
    }


def reference(query, cache_words, cache_scales, rowf, mix_words, mix_scales, offs, offs2, offs3, offs4, offs5):
    idx = unstriped8(offs)
    idx2 = unstriped8(offs2)
    idx3 = unstriped8(offs3)
    idx4 = unstriped8(offs4)
    idx5 = unstriped8(offs5)
    cacheu = unpack_weight(cache_words, cache_scales, "e4m3")
    mixu = unpack_weight(mix_words, mix_scales, "e2m1")
    queryq = mxq(f64(query), 0, "e4m3")
    a = queryq.T @ cacheu
    w = pick8(a, idx, 64) * 1.25
    w1 = np.pad(w, ((0, 0), (64, 0)))[:, :I]
    v = np.maximum(w1, pick8(a, idx2, 64))
    g = v - w
    gw = g * f64(rowf)
    gwq = mxq(gw, 0, "e4m3")
    o1 = mixu.T @ gwq
    pa = np.zeros((E, Z))
    pa[np.arange(E)[:, None], idx3[np.arange(E) % 128 // 16]] = o1
    pb = np.zeros((E, Z))
    pb[np.arange(E)[:, None], idx4[np.arange(E) % 128 // 16]] = o1
    m1 = np.minimum(pa, pb)
    y = pick8(m1, idx5, 16) + o1
    return y

@@ -1,0 +1,235 @@
+from contextlib import ExitStack
+
+import concourse.mybir as mybir
+
+D, T, Z, I, Q, E = 512, 1024, 1024, 512, 512, 256
+FLOPS = 2 * D * Q * T + 2 * Q * E * I
+
+F32 = mybir.dt.float32
+BF16 = mybir.dt.bfloat16
+I32 = mybir.dt.int32
+U32 = mybir.dt.uint32
+U16 = mybir.dt.uint16
+U8 = mybir.dt.uint8
+FP8X4 = mybir.dt.float8_e4m3fn_x4
+FP4X4 = mybir.dt.float4_e2m1fn_x4
+ALU = mybir.AluOpType
+COPY = mybir.ActivationFunctionType.Copy
+
+P = 128
+PACK = 4
+BANK = 512
+STEP_BACK = 64
+HALF = I // 2
+PART = 128
+SUB = 64
+LIST_ROWS = 16
+W_FACTOR = 1.25
+
+
+def list_slice(offsets, first, count):
+    return offsets[:, first // LIST_ROWS : (first + count) // LIST_ROWS]
+
+
+def spread_scale_rows(nc, plane, staged):
+    for quadrant in range(4):
+        nc.vector.tensor_copy(
+            out=plane[32 * quadrant : 32 * quadrant + 4, :].bitcast(I32),
+            in_=staged[:, quadrant, :],
+        )
+
+
+def tile_attend_stepback_one_postkept_kernel(
+    tc, query, cache_words, cache_scales, rowf, mix_words, mix_scales, offs, offs2, offs3, offs4, offs5, out
+):
+    nc = tc.nc
+    with ExitStack() as ctx:
+        held = ctx.enter_context(tc.tile_pool(name="held", bufs=1))
+        work = ctx.enter_context(tc.tile_pool(name="work", bufs=1))
+        score_psum = ctx.enter_context(tc.psum_pool(name="score_psum", bufs=4))
+        mix_psum = ctx.enter_context(tc.psum_pool(name="mix_psum", bufs=2))
+
+        cache_rows = held.tile([4, 4, T // 4], I32)
+        nc.sync.dma_start(out=cache_rows[:], in_=cache_scales[0].bitcast(I32).rearrange("(g j) c -> j g c", j=4))
+        mix_rows = held.tile([4, 4, E // 4], I32)
+        nc.sync.dma_start(out=mix_rows[:], in_=mix_scales[0].bitcast(I32).rearrange("(g j) c -> j g c", j=4))
+        query_rows = query.rearrange("(p t) q -> p t q", t=PACK)
+        query_raw = []
+        for h in range(2):
+            raw = held.tile([P, PACK, Q // 2], F32, name="query_raw%d" % h)
+            nc.sync.dma_start(out=raw[:], in_=query_rows[:, :, h * (Q // 2) : (h + 1) * (Q // 2)])
+            query_raw.append(raw)
+        cache_hbm = cache_words[0].rearrange("p n t -> p (n t)").bitcast(I32)
+        cache_codes = []
+        for b in range(T // BANK):
+            codes = work.tile([P, BANK], U32, name="cache_codes%d" % b, tag="slot_cache%d" % b, align_bytes=64)
+            nc.sync.dma_start(out=codes[:].bitcast(I32), in_=cache_hbm[:, b * BANK : (b + 1) * BANK])
+            cache_codes.append(codes)
+        lists = []
+        for n, source in enumerate((offs, offs2, offs3, offs4, offs5)):
+            lists.append(held.tile([P, I // LIST_ROWS], U16, name="list%d" % n))
+        list_w, list_v, list_a, list_b, list_out = lists
+        nc.sync.dma_start(list_w[:], offs)
+        nc.sync.dma_start(list_v[:], offs2)
+        row_factor = held.tile([P, PACK], F32)
+        nc.sync.dma_start(out=row_factor[:], in_=rowf.rearrange("(p r) o -> p (r o)", r=PACK))
+        mix_codes = held.tile([P, 2 * E], U8, align_bytes=64)
+        nc.sync.dma_start(out=mix_codes[:].bitcast(I32), in_=mix_words[0].bitcast(I32))
+        nc.sync.dma_start(list_a[:], offs3)
+        nc.sync.dma_start(list_b[:], offs4)
+        nc.sync.dma_start(list_out[:], offs5)
+
+        cache_plane = held.tile([P, T], U8, align_bytes=64)
+        nc.vector.memset(cache_plane[:].bitcast(U32), 0)
+        mix_plane = held.tile([P, E], U8, align_bytes=64)
+        nc.vector.memset(mix_plane[:].bitcast(U32), 0)
+        w_low = held.tile([P, PACK, STEP_BACK + HALF], F32)
+        nc.vector.memset(w_low[:, :, 0:STEP_BACK], 0.0)
+        pages = []
+        for n in range(2 * (E // P)):
+            page = held.tile([P, Z], F32, name="page%d" % n)
+            nc.vector.memset(page[:], 0.0)
+            pages.append(page)
+        spread_scale_rows(nc, cache_plane, cache_rows)
+        spread_scale_rows(nc, mix_plane, mix_rows)
+
+        query_bf = held.tile([P, PACK, P, PACK], BF16, align_bytes=64)
+        for h in range(2):
+            dealt = query_bf[:, :, h * (P // 2) : (h + 1) * (P // 2), :].rearrange("p r m t -> p m t r")
+            plain = query_raw[h][:].rearrange("p t (m r) -> p m t r", r=PACK)
+            if h == 0:
+                nc.scalar.activation(dealt, plain, COPY)
+            else:
+                nc.vector.tensor_copy(out=dealt[:, :, :, 0], in_=plain[:, :, :, 0])
+                nc.scalar.activation(dealt[:, :, :, 1:PACK], plain[:, :, :, 1:PACK], COPY)
+        query_codes, query_plane = [], []
+        for r in range(PACK):
+            codes = held.tile([P, P], U32, name="query_codes%d" % r, align_bytes=64)
+            plane = held.tile([P, P], U8, name="query_plane%d" % r, align_bytes=64)
+            nc.vector.quantize_mx(
+                out=codes[:].bitcast(FP8X4), scales=plane[:], in_=query_bf[:, r].rearrange("p m t -> p (m t)")
+            )
+            query_codes.append(codes)
+            query_plane.append(plane)
+
+        v_low = held.tile([P, PACK, HALF], F32)
+        scores = []
+        for r in range(PACK):
+            score = held.tile([P, T], F32, name="score%d" % r)
+            for b in range(T // BANK):
+                bank = score_psum.tile([P, BANK], F32, name="score_bank")
+                nc.tensor.matmul_mx(
+                    out=bank[:],
+                    lhsT=query_codes[r][:].bitcast(FP8X4),
+                    lhsT_scale=query_plane[r][:],
+                    rhs=cache_codes[b][:].bitcast(FP8X4),
+                    rhs_scale=cache_plane[:, b * BANK : (b + 1) * BANK],
+                    start=True,
+                    stop=True,
+                )
+                if b == 0:
+                    nc.scalar.activation(score[:, 0:BANK], bank[:], COPY)
+                else:
+                    nc.vector.tensor_copy(out=score[:, BANK:T], in_=bank[:])
+            scores.append(score)
+            nc.vector.tensor_scalar(
+                w_low[:, r, STEP_BACK:], score[:].indirect(list_slice(list_w, 0, HALF)), W_FACTOR, 0.0, ALU.mult, ALU.add
+            )
+            nc.scalar.activation(v_low[:, r, :], score[:].indirect(list_slice(list_v, 0, HALF)), COPY)
+
+        v_high = work.tile([P, PACK, HALF], F32, tag="slot_cache1", align_bytes=64)
+        for r in range(PACK):
+            nc.scalar.activation(v_high[:, r, :], scores[r][:].indirect(list_slice(list_v, HALF, HALF)), COPY)
+
+        mixed = [held.tile([P, E // P, HALF], F32, name="mixed%d" % h) for h in range(2)]
+        factor = row_factor[:].unsqueeze(1).unsqueeze(3).to_broadcast([P, SUB // 4, PACK, 4])
+
+        def scatter(e, n, first, count):
+            h, at = divmod(first, HALF)
+            nc.scalar.activation(
+                pages[2 * e + n][:].indirect(list_slice((list_a, list_b)[n], first, count)),
+                mixed[h][:, e, at : at + count],
+                COPY,
+            )
+
+        def part(s, w_half, v_half):
+            h, first = divmod(s * PART, HALF)
+            subs = [first + k * SUB for k in range(PART // SUB)]
+            larger = [work.tile([P, PACK, SUB], F32, name="larger%d_%d" % (s, k)) for k in range(len(subs))]
+            g = [work.tile([P, PACK, SUB], F32, name="g%d_%d" % (s, k)) for k in range(len(subs))]
+            gw_bf = work.tile([P, PART, PACK], BF16, name="gw_bf%d" % s, tag="slot_gw%d" % s, align_bytes=64)
+            for k, at in enumerate(subs):
+                nc.vector.tensor_tensor(
+                    larger[k][:], w_half[:, :, at : at + SUB], v_half[:, :, at : at + SUB], ALU.max
+                )
+            for k, at in enumerate(subs):
+                nc.vector.tensor_tensor(
+                    g[k][:], larger[k][:], w_half[:, :, STEP_BACK + at : STEP_BACK + at + SUB], ALU.subtract
+                )
+            for k in range(len(subs)):
+                nc.vector.tensor_tensor(
+                    gw_bf[:, k * SUB : (k + 1) * SUB, :].rearrange("p (c j) r -> p c r j", j=4),
+                    g[k][:].rearrange("p r (c j) -> p c r j", j=4),
+                    factor,
+                    ALU.mult,
+                )
+            gw_codes = work.tile([P, PART], U32, name="gw_codes%d" % s, align_bytes=64)
+            gw_plane = work.tile([P, PART], U8, name="gw_plane%d" % s, align_bytes=64)
+            nc.vector.quantize_mx(
+                out=gw_codes[:].bitcast(FP8X4), scales=gw_plane[:], in_=gw_bf[:].rearrange("p i r -> p (i r)")
+            )
+            bank = mix_psum.tile([P, E // P, PART], F32, name="mix_bank")
+            for e in range(E // P):
+                nc.tensor.matmul_mx(
+                    out=bank[:, e, :],
+                    lhsT=mix_codes[:, 2 * P * e : 2 * P * (e + 1)].bitcast(FP4X4),
+                    lhsT_scale=mix_plane[:, P * e : P * (e + 1)],
+                    rhs=gw_codes[:].bitcast(FP8X4),
+                    rhs_scale=gw_plane[:],
+                    start=True,
+                    stop=True,
+                )
+            target = mixed[h][:, :, first : first + PART]
+            if s == 0:
+                nc.scalar.activation(target, bank[:], COPY)
+            else:
+                nc.vector.tensor_copy(out=target, in_=bank[:])
+
+        for s in range(2):
+            part(s, w_low, v_low)
+            for e in range(E // P):
+                for n in range(2):
+                    scatter(e, n, s * PART, PART)
+        w_high = work.tile([P, PACK, STEP_BACK + HALF], F32, tag="slot_gw0", align_bytes=64)
+        nc.scalar.activation(
+            w_high[:, 0, STEP_BACK:], scores[0][:].indirect(list_slice(list_w, HALF, HALF)), COPY, scale=W_FACTOR
+        )
+        for r in range(1, PACK):
+            nc.vector.tensor_scalar(
+                w_high[:, r, STEP_BACK:],
+                scores[r][:].indirect(list_slice(list_w, HALF, HALF)),
+                W_FACTOR,
+                0.0,
+                ALU.mult,
+                ALU.add,
+            )
+        nc.vector.tensor_copy(out=w_high[:, :, 0:STEP_BACK], in_=w_low[:, :, HALF:])
+        part(2, w_high, v_high)
+        scatter(0, 0, 2 * PART, PART)
+        scatter(0, 1, 2 * PART, PART)
+        scatter(1, 0, 2 * PART, PART)
+        part(3, w_high, v_high)
+        scatter(0, 0, 3 * PART, PART)
+        scatter(0, 1, 3 * PART, PART)
+        scatter(1, 0, 3 * PART, PART)
+        scatter(1, 1, HALF, HALF)
+
+        for e in range(E // P):
+            lower = held.tile([P, Z], F32, name="lower%d" % e)
+            nc.vector.tensor_tensor(lower[:], pages[2 * e][:], pages[2 * e + 1][:], ALU.min)
+            for h in range(2):
+                result = held.tile([P, HALF], F32, name="result%d_%d" % (e, h))
+                nc.vector.tensor_tensor(
+                    result[:], lower[:].indirect(list_slice(list_out, h * HALF, HALF)), mixed[h][:, e, :], ALU.add
+                )
+                nc.sync.dma_start(out=out[e * P : (e + 1) * P, h * HALF : (h + 1) * HALF], in_=result[:])

@@ -46,13 +46,13 @@ def tile_attend_stepback_one_postkept_kernel(
     with ExitStack() as ctx:
         held = ctx.enter_context(tc.tile_pool(name="held", bufs=1))
         work = ctx.enter_context(tc.tile_pool(name="work", bufs=1))
-        score_psum = ctx.enter_context(tc.psum_pool(name="score_psum", bufs=4))
+        score_psum = ctx.enter_context(tc.psum_pool(name="score_psum", bufs=6))
         mix_psum = ctx.enter_context(tc.psum_pool(name="mix_psum", bufs=2))
 
         cache_rows = held.tile([4, 4, T // 4], I32)
-        nc.sync.dma_start(out=cache_rows[:], in_=cache_scales[0].bitcast(I32).rearrange("(g j) c -> j g c", j=4))
+        nc.scalar.dma_start(out=cache_rows[:], in_=cache_scales[0].bitcast(I32).rearrange("(g j) c -> j g c", j=4))
         mix_rows = held.tile([4, 4, E // 4], I32)
-        nc.sync.dma_start(out=mix_rows[:], in_=mix_scales[0].bitcast(I32).rearrange("(g j) c -> j g c", j=4))
+        nc.scalar.dma_start(out=mix_rows[:], in_=mix_scales[0].bitcast(I32).rearrange("(g j) c -> j g c", j=4))
         query_rows = query.rearrange("(p t) q -> p t q", t=PACK)
         query_raw = []
         for h in range(2):
@@ -62,7 +62,7 @@ def tile_attend_stepback_one_postkept_kernel(
         cache_hbm = cache_words[0].rearrange("p n t -> p (n t)").bitcast(I32)
         cache_codes = []
         for b in range(T // BANK):
-            codes = work.tile([P, BANK], U32, name="cache_codes%d" % b, tag="slot_cache%d" % b, align_bytes=64)
+            codes = work.tile([P, BANK], U32, name="cache_codes%d" % b, align_bytes=64)
             nc.sync.dma_start(out=codes[:].bitcast(I32), in_=cache_hbm[:, b * BANK : (b + 1) * BANK])
             cache_codes.append(codes)
         lists = []
@@ -83,63 +83,71 @@ def tile_attend_stepback_one_postkept_kernel(
         nc.vector.memset(cache_plane[:].bitcast(U32), 0)
         mix_plane = held.tile([P, E], U8, align_bytes=64)
         nc.vector.memset(mix_plane[:].bitcast(U32), 0)
-        w_low = held.tile([P, PACK, STEP_BACK + HALF], F32)
-        nc.vector.memset(w_low[:, :, 0:STEP_BACK], 0.0)
+        spread_scale_rows(nc, cache_plane, cache_rows)
+        spread_scale_rows(nc, mix_plane, mix_rows)
         pages = []
         for n in range(2 * (E // P)):
             page = held.tile([P, Z], F32, name="page%d" % n)
-            nc.vector.memset(page[:], 0.0)
+            nc.vector.memset(page[:].bitcast(I32), 0)
             pages.append(page)
-        spread_scale_rows(nc, cache_plane, cache_rows)
-        spread_scale_rows(nc, mix_plane, mix_rows)
 
-        query_bf = held.tile([P, PACK, P, PACK], BF16, align_bytes=64)
+        first_bf = held.tile([P, P, PACK], BF16, align_bytes=64)
+        rest_bf = held.tile([P, PACK - 1, P, PACK], BF16, align_bytes=64)
         for h in range(2):
-            dealt = query_bf[:, :, h * (P // 2) : (h + 1) * (P // 2), :].rearrange("p r m t -> p m t r")
+            columns = slice(h * (P // 2), (h + 1) * (P // 2))
             plain = query_raw[h][:].rearrange("p t (m r) -> p m t r", r=PACK)
-            if h == 0:
-                nc.scalar.activation(dealt, plain, COPY)
-            else:
-                nc.vector.tensor_copy(out=dealt[:, :, :, 0], in_=plain[:, :, :, 0])
-                nc.scalar.activation(dealt[:, :, :, 1:PACK], plain[:, :, :, 1:PACK], COPY)
+            nc.vector.tensor_copy(out=first_bf[:, columns, :], in_=plain[:, :, :, 0])
+            nc.scalar.activation(
+                rest_bf[:, :, columns, :].rearrange("p r m t -> p m t r"), plain[:, :, :, 1:PACK], COPY
+            )
+        query_bf = [first_bf[:]] + [rest_bf[:, r] for r in range(PACK - 1)]
+        rows = held.tile([P, PACK, 2 * HALF - SUB], F32)
+        w_high = rows[:, :, 0:HALF]
+        v_low = rows[:, :, HALF - SUB : 2 * HALF - SUB]
+        w_low = held.tile([P, PACK, HALF], F32)
         query_codes, query_plane = [], []
         for r in range(PACK):
             codes = held.tile([P, P], U32, name="query_codes%d" % r, align_bytes=64)
             plane = held.tile([P, P], U8, name="query_plane%d" % r, align_bytes=64)
             nc.vector.quantize_mx(
-                out=codes[:].bitcast(FP8X4), scales=plane[:], in_=query_bf[:, r].rearrange("p m t -> p (m t)")
+                out=codes[:].bitcast(FP8X4), scales=plane[:], in_=query_bf[r].rearrange("p m t -> p (m t)")
             )
             query_codes.append(codes)
             query_plane.append(plane)
 
-        v_low = held.tile([P, PACK, HALF], F32)
         scores = []
+
+        def look_up_low(r):
+            nc.scalar.activation(
+                w_low[:, r, :], scores[r][:].indirect(list_slice(list_w, 0, HALF)), COPY, scale=W_FACTOR
+            )
+            nc.vector.tensor_copy(out=v_low[:, r, :], in_=scores[r][:].indirect(list_slice(list_v, 0, HALF)))
+
         for r in range(PACK):
             score = held.tile([P, T], F32, name="score%d" % r)
-            for b in range(T // BANK):
+            width = BANK // 2 if r == 0 else BANK
+            for n, first in enumerate(range(0, T, width)):
+                b, at = divmod(first, BANK)
                 bank = score_psum.tile([P, BANK], F32, name="score_bank")
                 nc.tensor.matmul_mx(
-                    out=bank[:],
+                    out=bank[:, 0:width],
                     lhsT=query_codes[r][:].bitcast(FP8X4),
                     lhsT_scale=query_plane[r][:],
-                    rhs=cache_codes[b][:].bitcast(FP8X4),
-                    rhs_scale=cache_plane[:, b * BANK : (b + 1) * BANK],
+                    rhs=cache_codes[b][:, at : at + width].bitcast(FP8X4),
+                    rhs_scale=cache_plane[:, first : first + width],
                     start=True,
                     stop=True,
                 )
-                if b == 0:
-                    nc.scalar.activation(score[:, 0:BANK], bank[:], COPY)
+                if (n + (r == 2)) % 2 == 0:
+                    nc.scalar.activation(score[:, first : first + width], bank[:, 0:width], COPY)
                 else:
-                    nc.vector.tensor_copy(out=score[:, BANK:T], in_=bank[:])
+                    nc.vector.tensor_copy(out=score[:, first : first + width], in_=bank[:, 0:width])
             scores.append(score)
-            nc.vector.tensor_scalar(
-                w_low[:, r, STEP_BACK:], score[:].indirect(list_slice(list_w, 0, HALF)), W_FACTOR, 0.0, ALU.mult, ALU.add
-            )
-            nc.scalar.activation(v_low[:, r, :], score[:].indirect(list_slice(list_v, 0, HALF)), COPY)
-
-        v_high = work.tile([P, PACK, HALF], F32, tag="slot_cache1", align_bytes=64)
-        for r in range(PACK):
-            nc.scalar.activation(v_high[:, r, :], scores[r][:].indirect(list_slice(list_v, HALF, HALF)), COPY)
+            if r == 0:
+                look_up_low(0)
+            if r >= 2:
+                look_up_low(r - 1)
+        look_up_low(PACK - 1)
 
         mixed = [held.tile([P, E // P, HALF], F32, name="mixed%d" % h) for h in range(2)]
         factor = row_factor[:].unsqueeze(1).unsqueeze(3).to_broadcast([P, SUB // 4, PACK, 4])
@@ -152,36 +160,55 @@ def tile_attend_stepback_one_postkept_kernel(
                 COPY,
             )
 
-        def part(s, w_half, v_half):
+        def w_at(first):
+            return (w_low, w_high)[first // HALF][:, :, first % HALF : first % HALF + SUB]
+
+        def part(s, v_half):
             h, first = divmod(s * PART, HALF)
-            subs = [first + k * SUB for k in range(PART // SUB)]
-            larger = [work.tile([P, PACK, SUB], F32, name="larger%d_%d" % (s, k)) for k in range(len(subs))]
-            g = [work.tile([P, PACK, SUB], F32, name="g%d_%d" % (s, k)) for k in range(len(subs))]
             gw_bf = work.tile([P, PART, PACK], BF16, name="gw_bf%d" % s, tag="slot_gw%d" % s, align_bytes=64)
-            for k, at in enumerate(subs):
-                nc.vector.tensor_tensor(
-                    larger[k][:], w_half[:, :, at : at + SUB], v_half[:, :, at : at + SUB], ALU.max
-                )
-            for k, at in enumerate(subs):
-                nc.vector.tensor_tensor(
-                    g[k][:], larger[k][:], w_half[:, :, STEP_BACK + at : STEP_BACK + at + SUB], ALU.subtract
-                )
-            for k in range(len(subs)):
+            larger, g = {}, {}
+
+            def take_larger(k):
+                slot = s * PART + k * SUB
+                if slot >= STEP_BACK:
+                    tag = "slot_g%d" % (1 - k) if s == 1 else "larger%d_%d" % (s, k)
+                    larger[k] = work.tile([P, PACK, SUB], F32, name="larger%d_%d" % (s, k), tag=tag)
+                    at = first + k * SUB
+                    nc.vector.tensor_tensor(larger[k][:], w_at(slot - STEP_BACK), v_half[:, :, at : at + SUB], ALU.max)
+
+            def subtract(k):
+                slot = s * PART + k * SUB
+                tag = "slot_g%d" % k if s == 0 else "g%d_%d" % (s, k)
+                g[k] = work.tile([P, PACK, SUB], F32, name="g%d_%d" % (s, k), tag=tag)
+                if slot >= STEP_BACK:
+                    nc.vector.tensor_tensor(g[k][:], larger[k][:], w_at(slot), ALU.subtract)
+                else:
+                    nc.vector.scalar_tensor_tensor(g[k][:], v_half[:, :, 0:SUB], 0.0, w_at(slot), ALU.max, ALU.subtract)
+
+            def weigh(k):
                 nc.vector.tensor_tensor(
                     gw_bf[:, k * SUB : (k + 1) * SUB, :].rearrange("p (c j) r -> p c r j", j=4),
                     g[k][:].rearrange("p r (c j) -> p c r j", j=4),
                     factor,
                     ALU.mult,
                 )
+
+            if s == 0:
+                for step, k in ((subtract, 0), (take_larger, 1), (weigh, 0), (subtract, 1), (weigh, 1)):
+                    step(k)
+            else:
+                for step in (take_larger, subtract, weigh):
+                    for k in range(PART // SUB):
+                        step(k)
             gw_codes = work.tile([P, PART], U32, name="gw_codes%d" % s, align_bytes=64)
             gw_plane = work.tile([P, PART], U8, name="gw_plane%d" % s, align_bytes=64)
             nc.vector.quantize_mx(
                 out=gw_codes[:].bitcast(FP8X4), scales=gw_plane[:], in_=gw_bf[:].rearrange("p i r -> p (i r)")
             )
-            bank = mix_psum.tile([P, E // P, PART], F32, name="mix_bank")
+            banks = [mix_psum.tile([P, E // P, PART], F32, name="mix_bank") for e in range(E // P if s == 0 else 1)]
             for e in range(E // P):
                 nc.tensor.matmul_mx(
-                    out=bank[:, e, :],
+                    out=banks[e % len(banks)][:, e, :],
                     lhsT=mix_codes[:, 2 * P * e : 2 * P * (e + 1)].bitcast(FP4X4),
                     lhsT_scale=mix_plane[:, P * e : P * (e + 1)],
                     rhs=gw_codes[:].bitcast(FP8X4),
@@ -189,47 +216,44 @@ def tile_attend_stepback_one_postkept_kernel(
                     start=True,
                     stop=True,
                 )
-            target = mixed[h][:, :, first : first + PART]
             if s == 0:
-                nc.scalar.activation(target, bank[:], COPY)
+                nc.scalar.activation(mixed[h][:, 0, first : first + PART], banks[0][:, 0, :], COPY)
+                nc.vector.tensor_copy(out=mixed[h][:, 1, first : first + PART], in_=banks[1][:, 1, :])
             else:
-                nc.vector.tensor_copy(out=target, in_=bank[:])
+                nc.vector.tensor_copy(out=mixed[h][:, :, first : first + PART], in_=banks[0][:])
 
         for s in range(2):
-            part(s, w_low, v_low)
+            part(s, v_low)
+            if s == 0:
+                for r in range(PACK):
+                    nc.scalar.activation(
+                        w_high[:, r, :], scores[r][:].indirect(list_slice(list_w, HALF, HALF)), COPY, scale=W_FACTOR
+                    )
             for e in range(E // P):
                 for n in range(2):
                     scatter(e, n, s * PART, PART)
-        w_high = work.tile([P, PACK, STEP_BACK + HALF], F32, tag="slot_gw0", align_bytes=64)
-        nc.scalar.activation(
-            w_high[:, 0, STEP_BACK:], scores[0][:].indirect(list_slice(list_w, HALF, HALF)), COPY, scale=W_FACTOR
-        )
-        for r in range(1, PACK):
-            nc.vector.tensor_scalar(
-                w_high[:, r, STEP_BACK:],
-                scores[r][:].indirect(list_slice(list_w, HALF, HALF)),
-                W_FACTOR,
-                0.0,
-                ALU.mult,
-                ALU.add,
-            )
-        nc.vector.tensor_copy(out=w_high[:, :, 0:STEP_BACK], in_=w_low[:, :, HALF:])
-        part(2, w_high, v_high)
+        v_high = work.tile([P, PACK, HALF], F32, tag="slot_gw0", align_bytes=64)
+        for r in range(PACK):
+            nc.vector.tensor_copy(out=v_high[:, r, :], in_=scores[r][:].indirect(list_slice(list_v, HALF, HALF)))
+        part(2, v_high)
         scatter(0, 0, 2 * PART, PART)
         scatter(0, 1, 2 * PART, PART)
-        scatter(1, 0, 2 * PART, PART)
-        part(3, w_high, v_high)
+        scatter(1, 0, 2 * PART, SUB)
+        part(3, v_high)
         scatter(0, 0, 3 * PART, PART)
         scatter(0, 1, 3 * PART, PART)
-        scatter(1, 0, 3 * PART, PART)
+        scatter(1, 0, HALF + SUB, HALF - SUB)
         scatter(1, 1, HALF, HALF)
 
         for e in range(E // P):
-            lower = held.tile([P, Z], F32, name="lower%d" % e)
+            lower = held.tile([P, Z], F32, name="lower")
             nc.vector.tensor_tensor(lower[:], pages[2 * e][:], pages[2 * e + 1][:], ALU.min)
             for h in range(2):
                 result = held.tile([P, HALF], F32, name="result%d_%d" % (e, h))
-                nc.vector.tensor_tensor(
-                    result[:], lower[:].indirect(list_slice(list_out, h * HALF, HALF)), mixed[h][:, e, :], ALU.add
-                )
+                picked = lower[:].indirect(list_slice(list_out, h * HALF, HALF))
+                if e == 1 and h == 1:
+                    looked_up = held.tile([P, HALF], F32)
+                    nc.scalar.activation(looked_up[:], picked, COPY)
+                    picked = looked_up[:]
+                nc.vector.tensor_tensor(result[:], picked, mixed[h][:, e, :], ALU.add)
                 nc.sync.dma_start(out=out[e * P : (e + 1) * P, h * HALF : (h + 1) * HALF], in_=result[:])

@@ -50,9 +50,9 @@ def tile_attend_stepback_one_postkept_kernel(
         mix_psum = ctx.enter_context(tc.psum_pool(name="mix_psum", bufs=2))
 
         cache_rows = held.tile([4, 4, T // 4], I32)
-        nc.scalar.dma_start(out=cache_rows[:], in_=cache_scales[0].bitcast(I32).rearrange("(g j) c -> j g c", j=4))
+        nc.sync.dma_start(out=cache_rows[:], in_=cache_scales[0].bitcast(I32).rearrange("(g j) c -> j g c", j=4))
         mix_rows = held.tile([4, 4, E // 4], I32)
-        nc.scalar.dma_start(out=mix_rows[:], in_=mix_scales[0].bitcast(I32).rearrange("(g j) c -> j g c", j=4))
+        nc.sync.dma_start(out=mix_rows[:], in_=mix_scales[0].bitcast(I32).rearrange("(g j) c -> j g c", j=4))
         query_rows = query.rearrange("(p t) q -> p t q", t=PACK)
         query_raw = []
         for h in range(2):
@@ -83,13 +83,13 @@ def tile_attend_stepback_one_postkept_kernel(
         nc.vector.memset(cache_plane[:].bitcast(U32), 0)
         mix_plane = held.tile([P, E], U8, align_bytes=64)
         nc.vector.memset(mix_plane[:].bitcast(U32), 0)
-        spread_scale_rows(nc, cache_plane, cache_rows)
-        spread_scale_rows(nc, mix_plane, mix_rows)
         pages = []
         for n in range(2 * (E // P)):
             page = held.tile([P, Z], F32, name="page%d" % n)
             nc.vector.memset(page[:].bitcast(I32), 0)
             pages.append(page)
+        spread_scale_rows(nc, cache_plane, cache_rows)
+        spread_scale_rows(nc, mix_plane, mix_rows)
 
         first_bf = held.tile([P, P, PACK], BF16, align_bytes=64)
         rest_bf = held.tile([P, PACK - 1, P, PACK], BF16, align_bytes=64)

@@ -51,13 +51,11 @@ def tile_attend_stepback_one_postkept_kernel(
 
         cache_rows = held.tile([4, 4, T // 4], I32)
         nc.sync.dma_start(out=cache_rows[:], in_=cache_scales[0].bitcast(I32).rearrange("(g j) c -> j g c", j=4))
-        mix_rows = held.tile([4, 4, E // 4], I32)
-        nc.sync.dma_start(out=mix_rows[:], in_=mix_scales[0].bitcast(I32).rearrange("(g j) c -> j g c", j=4))
         query_rows = query.rearrange("(p t) q -> p t q", t=PACK)
         query_raw = []
         for h in range(2):
-            raw = held.tile([P, PACK, Q // 2], F32, name="query_raw%d" % h)
-            nc.sync.dma_start(out=raw[:], in_=query_rows[:, :, h * (Q // 2) : (h + 1) * (Q // 2)])
+            raw = held.tile([P, 2, Q], F32, name="query_raw%d" % h)
+            nc.sync.dma_start(out=raw[:], in_=query_rows[:, 2 * h : 2 * h + 2, :])
             query_raw.append(raw)
         cache_hbm = cache_words[0].rearrange("p n t -> p (n t)").bitcast(I32)
         cache_codes = []
@@ -75,30 +73,32 @@ def tile_attend_stepback_one_postkept_kernel(
         nc.sync.dma_start(out=row_factor[:], in_=rowf.rearrange("(p r) o -> p (r o)", r=PACK))
         mix_codes = held.tile([P, 2 * E], U8, align_bytes=64)
         nc.sync.dma_start(out=mix_codes[:].bitcast(I32), in_=mix_words[0].bitcast(I32))
+        mix_plane = held.tile([P, E], U8, align_bytes=64)
+        nc.vector.memset(mix_plane[:].bitcast(U32), 0)
+        mix_rows = mix_scales[0].bitcast(I32).rearrange("(g j) c -> j g c", j=4)
+        for j in range(4):
+            nc.sync.dma_start(out=mix_plane[j:P:32, :].bitcast(I32), in_=mix_rows[j])
         nc.sync.dma_start(list_a[:], offs3)
         nc.sync.dma_start(list_b[:], offs4)
         nc.sync.dma_start(list_out[:], offs5)
 
         cache_plane = held.tile([P, T], U8, align_bytes=64)
         nc.vector.memset(cache_plane[:].bitcast(U32), 0)
-        mix_plane = held.tile([P, E], U8, align_bytes=64)
-        nc.vector.memset(mix_plane[:].bitcast(U32), 0)
         pages = []
         for n in range(2 * (E // P)):
             page = held.tile([P, Z], F32, name="page%d" % n)
             nc.vector.memset(page[:].bitcast(I32), 0)
             pages.append(page)
         spread_scale_rows(nc, cache_plane, cache_rows)
-        spread_scale_rows(nc, mix_plane, mix_rows)
 
         first_bf = held.tile([P, P, PACK], BF16, align_bytes=64)
         rest_bf = held.tile([P, PACK - 1, P, PACK], BF16, align_bytes=64)
         for h in range(2):
-            columns = slice(h * (P // 2), (h + 1) * (P // 2))
+            places = slice(2 * h, 2 * h + 2)
             plain = query_raw[h][:].rearrange("p t (m r) -> p m t r", r=PACK)
-            nc.vector.tensor_copy(out=first_bf[:, columns, :], in_=plain[:, :, :, 0])
+            nc.vector.tensor_copy(out=first_bf[:, :, places], in_=plain[:, :, :, 0])
             nc.scalar.activation(
-                rest_bf[:, :, columns, :].rearrange("p r m t -> p m t r"), plain[:, :, :, 1:PACK], COPY
+                rest_bf[:, :, :, places].rearrange("p r m t -> p m t r"), plain[:, :, :, 1:PACK], COPY
             )
         query_bf = [first_bf[:]] + [rest_bf[:, r] for r in range(PACK - 1)]
         rows = held.tile([P, PACK, 2 * HALF - SUB], F32)
@@ -238,11 +238,10 @@ def tile_attend_stepback_one_postkept_kernel(
         part(2, v_high)
         scatter(0, 0, 2 * PART, PART)
         scatter(0, 1, 2 * PART, PART)
-        scatter(1, 0, 2 * PART, SUB)
         part(3, v_high)
         scatter(0, 0, 3 * PART, PART)
         scatter(0, 1, 3 * PART, PART)
-        scatter(1, 0, HALF + SUB, HALF - SUB)
+        scatter(1, 0, HALF, HALF)
         scatter(1, 1, HALF, HALF)
 
         for e in range(E // P):

from contextlib import ExitStack

import concourse.mybir as mybir

D, T, Z, I, Q, E = 512, 1024, 1024, 512, 512, 256
FLOPS = 2 * D * Q * T + 2 * Q * E * I

F32 = mybir.dt.float32
BF16 = mybir.dt.bfloat16
I32 = mybir.dt.int32
U32 = mybir.dt.uint32
U16 = mybir.dt.uint16
U8 = mybir.dt.uint8
FP8X4 = mybir.dt.float8_e4m3fn_x4
FP4X4 = mybir.dt.float4_e2m1fn_x4
ALU = mybir.AluOpType
COPY = mybir.ActivationFunctionType.Copy

P = 128
PACK = 4
BANK = 512
STEP_BACK = 64
HALF = I // 2
PART = 128
SUB = 64
LIST_ROWS = 16
W_FACTOR = 1.25


def list_slice(offsets, first, count):
    return offsets[:, first // LIST_ROWS : (first + count) // LIST_ROWS]


def spread_scale_rows(nc, plane, staged):
    for quadrant in range(4):
        nc.vector.tensor_copy(
            out=plane[32 * quadrant : 32 * quadrant + 4, :].bitcast(I32),
            in_=staged[:, quadrant, :],
        )


def tile_attend_stepback_one_postkept_kernel(
    tc, query, cache_words, cache_scales, rowf, mix_words, mix_scales, offs, offs2, offs3, offs4, offs5, out
):
    nc = tc.nc
    with ExitStack() as ctx:
        held = ctx.enter_context(tc.tile_pool(name="held", bufs=1))
        work = ctx.enter_context(tc.tile_pool(name="work", bufs=1))
        score_psum = ctx.enter_context(tc.psum_pool(name="score_psum", bufs=6))
        mix_psum = ctx.enter_context(tc.psum_pool(name="mix_psum", bufs=2))

        cache_rows = held.tile([4, 4, T // 4], I32)
        nc.sync.dma_start(out=cache_rows[:], in_=cache_scales[0].bitcast(I32).rearrange("(g j) c -> j g c", j=4))
        query_rows = query.rearrange("(p t) q -> p t q", t=PACK)
        query_raw = []
        for h in range(2):
            raw = held.tile([P, 2, Q], F32, name="query_raw%d" % h)
            nc.sync.dma_start(out=raw[:], in_=query_rows[:, 2 * h : 2 * h + 2, :])
            query_raw.append(raw)
        cache_hbm = cache_words[0].rearrange("p n t -> p (n t)").bitcast(I32)
        cache_codes = []
        for b in range(T // BANK):
            codes = work.tile([P, BANK], U32, name="cache_codes%d" % b, align_bytes=64)
            nc.sync.dma_start(out=codes[:].bitcast(I32), in_=cache_hbm[:, b * BANK : (b + 1) * BANK])
            cache_codes.append(codes)
        lists = []
        for n, source in enumerate((offs, offs2, offs3, offs4, offs5)):
            lists.append(held.tile([P, I // LIST_ROWS], U16, name="list%d" % n))
        list_w, list_v, list_a, list_b, list_out = lists
        nc.sync.dma_start(list_w[:], offs)
        nc.sync.dma_start(list_v[:], offs2)
        row_factor = held.tile([P, PACK], F32)
        nc.sync.dma_start(out=row_factor[:], in_=rowf.rearrange("(p r) o -> p (r o)", r=PACK))
        mix_codes = held.tile([P, 2 * E], U8, align_bytes=64)
        nc.sync.dma_start(out=mix_codes[:].bitcast(I32), in_=mix_words[0].bitcast(I32))
        mix_plane = held.tile([P, E], U8, align_bytes=64)
        nc.vector.memset(mix_plane[:].bitcast(U32), 0)
        mix_rows = mix_scales[0].bitcast(I32).rearrange("(g j) c -> j g c", j=4)
        for j in range(4):
            nc.sync.dma_start(out=mix_plane[j:P:32, :].bitcast(I32), in_=mix_rows[j])
        nc.sync.dma_start(list_a[:], offs3)
        nc.sync.dma_start(list_b[:], offs4)
        nc.sync.dma_start(list_out[:], offs5)

        cache_plane = held.tile([P, T], U8, align_bytes=64)
        nc.vector.memset(cache_plane[:].bitcast(U32), 0)
        pages = []
        for n in range(2 * (E // P)):
            page = held.tile([P, Z], F32, name="page%d" % n)
            nc.vector.memset(page[:].bitcast(I32), 0)
            pages.append(page)
        spread_scale_rows(nc, cache_plane, cache_rows)

        first_bf = held.tile([P, P, PACK], BF16, align_bytes=64)
        rest_bf = held.tile([P, PACK - 1, P, PACK], BF16, align_bytes=64)
        for h in range(2):
            places = slice(2 * h, 2 * h + 2)
            plain = query_raw[h][:].rearrange("p t (m r) -> p m t r", r=PACK)
            nc.vector.tensor_copy(out=first_bf[:, :, places], in_=plain[:, :, :, 0])
            nc.scalar.activation(
                rest_bf[:, :, :, places].rearrange("p r m t -> p m t r"), plain[:, :, :, 1:PACK], COPY
            )
        query_bf = [first_bf[:]] + [rest_bf[:, r] for r in range(PACK - 1)]
        rows = held.tile([P, PACK, 2 * HALF - SUB], F32)
        w_high = rows[:, :, 0:HALF]
        v_low = rows[:, :, HALF - SUB : 2 * HALF - SUB]
        w_low = held.tile([P, PACK, HALF], F32)
        query_codes, query_plane = [], []
        for r in range(PACK):
            codes = held.tile([P, P], U32, name="query_codes%d" % r, align_bytes=64)
            plane = held.tile([P, P], U8, name="query_plane%d" % r, align_bytes=64)
            nc.vector.quantize_mx(
                out=codes[:].bitcast(FP8X4), scales=plane[:], in_=query_bf[r].rearrange("p m t -> p (m t)")
            )
            query_codes.append(codes)
            query_plane.append(plane)

        scores = []

        def look_up_low(r):
            nc.scalar.activation(
                w_low[:, r, :], scores[r][:].indirect(list_slice(list_w, 0, HALF)), COPY, scale=W_FACTOR
            )
            nc.vector.tensor_copy(out=v_low[:, r, :], in_=scores[r][:].indirect(list_slice(list_v, 0, HALF)))

        for r in range(PACK):
            score = held.tile([P, T], F32, name="score%d" % r)
            width = BANK // 2 if r == 0 else BANK
            for n, first in enumerate(range(0, T, width)):
                b, at = divmod(first, BANK)
                bank = score_psum.tile([P, BANK], F32, name="score_bank")
                nc.tensor.matmul_mx(
                    out=bank[:, 0:width],
                    lhsT=query_codes[r][:].bitcast(FP8X4),
                    lhsT_scale=query_plane[r][:],
                    rhs=cache_codes[b][:, at : at + width].bitcast(FP8X4),
                    rhs_scale=cache_plane[:, first : first + width],
                    start=True,
                    stop=True,
                )
                if (n + (r == 2)) % 2 == 0:
                    nc.scalar.activation(score[:, first : first + width], bank[:, 0:width], COPY)
                else:
                    nc.vector.tensor_copy(out=score[:, first : first + width], in_=bank[:, 0:width])
            scores.append(score)
            if r == 0:
                look_up_low(0)
            if r >= 2:
                look_up_low(r - 1)
        look_up_low(PACK - 1)

        mixed = [held.tile([P, E // P, HALF], F32, name="mixed%d" % h) for h in range(2)]
        factor = row_factor[:].unsqueeze(1).unsqueeze(3).to_broadcast([P, SUB // 4, PACK, 4])

        def scatter(e, n, first, count):
            h, at = divmod(first, HALF)
            nc.scalar.activation(
                pages[2 * e + n][:].indirect(list_slice((list_a, list_b)[n], first, count)),
                mixed[h][:, e, at : at + count],
                COPY,
            )

        def w_at(first):
            return (w_low, w_high)[first // HALF][:, :, first % HALF : first % HALF + SUB]

        def part(s, v_half):
            h, first = divmod(s * PART, HALF)
            gw_bf = work.tile([P, PART, PACK], BF16, name="gw_bf%d" % s, tag="slot_gw%d" % s, align_bytes=64)
            larger, g = {}, {}

            def take_larger(k):
                slot = s * PART + k * SUB
                if slot >= STEP_BACK:
                    tag = "slot_g%d" % (1 - k) if s == 1 else "larger%d_%d" % (s, k)
                    larger[k] = work.tile([P, PACK, SUB], F32, name="larger%d_%d" % (s, k), tag=tag)
                    at = first + k * SUB
                    nc.vector.tensor_tensor(larger[k][:], w_at(slot - STEP_BACK), v_half[:, :, at : at + SUB], ALU.max)

            def subtract(k):
                slot = s * PART + k * SUB
                tag = "slot_g%d" % k if s == 0 else "g%d_%d" % (s, k)
                g[k] = work.tile([P, PACK, SUB], F32, name="g%d_%d" % (s, k), tag=tag)
                if slot >= STEP_BACK:
                    nc.vector.tensor_tensor(g[k][:], larger[k][:], w_at(slot), ALU.subtract)
                else:
                    nc.vector.scalar_tensor_tensor(g[k][:], v_half[:, :, 0:SUB], 0.0, w_at(slot), ALU.max, ALU.subtract)

            def weigh(k):
                nc.vector.tensor_tensor(
                    gw_bf[:, k * SUB : (k + 1) * SUB, :].rearrange("p (c j) r -> p c r j", j=4),
                    g[k][:].rearrange("p r (c j) -> p c r j", j=4),
                    factor,
                    ALU.mult,
                )

            if s == 0:
                for step, k in ((subtract, 0), (take_larger, 1), (weigh, 0), (subtract, 1), (weigh, 1)):
                    step(k)
            else:
                for step in (take_larger, subtract, weigh):
                    for k in range(PART // SUB):
                        step(k)
            gw_codes = work.tile([P, PART], U32, name="gw_codes%d" % s, align_bytes=64)
            gw_plane = work.tile([P, PART], U8, name="gw_plane%d" % s, align_bytes=64)
            nc.vector.quantize_mx(
                out=gw_codes[:].bitcast(FP8X4), scales=gw_plane[:], in_=gw_bf[:].rearrange("p i r -> p (i r)")
            )
            banks = [mix_psum.tile([P, E // P, PART], F32, name="mix_bank") for e in range(E // P if s == 0 else 1)]
            for e in range(E // P):
                nc.tensor.matmul_mx(
                    out=banks[e % len(banks)][:, e, :],
                    lhsT=mix_codes[:, 2 * P * e : 2 * P * (e + 1)].bitcast(FP4X4),
                    lhsT_scale=mix_plane[:, P * e : P * (e + 1)],
                    rhs=gw_codes[:].bitcast(FP8X4),
                    rhs_scale=gw_plane[:],
                    start=True,
                    stop=True,
                )
            if s == 0:
                nc.scalar.activation(mixed[h][:, 0, first : first + PART], banks[0][:, 0, :], COPY)
                nc.vector.tensor_copy(out=mixed[h][:, 1, first : first + PART], in_=banks[1][:, 1, :])
            else:
                nc.vector.tensor_copy(out=mixed[h][:, :, first : first + PART], in_=banks[0][:])

        for s in range(2):
            part(s, v_low)
            if s == 0:
                for r in range(PACK):
                    nc.scalar.activation(
                        w_high[:, r, :], scores[r][:].indirect(list_slice(list_w, HALF, HALF)), COPY, scale=W_FACTOR
                    )
            for e in range(E // P):
                for n in range(2):
                    scatter(e, n, s * PART, PART)
        v_high = work.tile([P, PACK, HALF], F32, tag="slot_gw0", align_bytes=64)
        for r in range(PACK):
            nc.vector.tensor_copy(out=v_high[:, r, :], in_=scores[r][:].indirect(list_slice(list_v, HALF, HALF)))
        part(2, v_high)
        scatter(0, 0, 2 * PART, PART)
        scatter(0, 1, 2 * PART, PART)
        part(3, v_high)
        scatter(0, 0, 3 * PART, PART)
        scatter(0, 1, 3 * PART, PART)
        scatter(1, 0, HALF, HALF)
        scatter(1, 1, HALF, HALF)

        for e in range(E // P):
            lower = held.tile([P, Z], F32, name="lower")
            nc.vector.tensor_tensor(lower[:], pages[2 * e][:], pages[2 * e + 1][:], ALU.min)
            for h in range(2):
                result = held.tile([P, HALF], F32, name="result%d_%d" % (e, h))
                picked = lower[:].indirect(list_slice(list_out, h * HALF, HALF))
                if e == 1 and h == 1:
                    looked_up = held.tile([P, HALF], F32)
                    nc.scalar.activation(looked_up[:], picked, COPY)
                    picked = looked_up[:]
                nc.vector.tensor_tensor(result[:], picked, mixed[h][:, e, :], ALU.add)
                nc.sync.dma_start(out=out[e * P : (e + 1) * P, h * HALF : (h + 1) * HALF], in_=result[:])
